import numpy as np
import ml_dtypes


def mxq(x, axis, fmt="e4m3"):
    dtype, down = {"e4m3": (ml_dtypes.float8_e4m3fn, 7), "e5m2": (ml_dtypes.float8_e5m2, 14)}[fmt]
    v = np.moveaxis(np.asarray(x, np.float32).astype(ml_dtypes.bfloat16).astype(np.float64), axis, -1)
    blocks = v.reshape(v.shape[:-1] + (-1, 32))
    amax = np.abs(blocks).max(-1, keepdims=True)
    byte = np.maximum(np.where(amax > 0, np.frexp(amax)[1] - 1 + 127, 0) - down, 1)
    scale = np.exp2(byte - 127.0)
    codes = (blocks / scale).astype(np.float32).astype(dtype).astype(np.float64)
    return np.moveaxis((codes * scale).reshape(v.shape), -1, axis)


WIDE = False


def mx_kscale(k):
    if not WIDE:
        return np.ones(k)
    levels = np.array([10, -10, 5, -5, 0])
    if k % 512:
        return np.exp2(np.random.permutation(np.resize(levels, k // 32))).repeat(32)
    a = np.empty((k // 512, 16))
    for p in range(k // 512):
        a[p, :8] = np.random.permutation(np.resize(levels, 8))
        for g in range(8):
            far = levels[np.abs(levels - a[p, g]) >= 10]
            a[p, g + 8] = far[np.random.randint(len(far))]
    return np.exp2(a.ravel()).repeat(32)


def f64(x):
    return np.asarray(x).astype(np.float64)


def striped(idx):
    return np.tile(np.asarray(idx).reshape(-1, 16).T, (8, 1)).astype(np.uint16)


def unstriped(offs):
    return offs[:16].T.reshape(-1).astype(np.int64)


def striped8(idx):
    return np.asarray(idx).reshape(8, -1, 16).transpose(0, 2, 1).reshape(128, -1).astype(np.uint16)


def unstriped8(offs):
    return offs.reshape(8, 16, -1).transpose(0, 2, 1).reshape(8, -1).astype(np.int64)


def pick8(x, idx, run):
    r = np.arange(len(x))
    return x[r[:, None], idx[r % (8 * run) // run]]


E2M1 = np.array([0.0, 0.5, 1.0, 1.5, 2.0, 3.0, 4.0, 6.0, -0.0, -0.5, -1.0, -1.5, -2.0, -3.0, -4.0, -6.0])


def pack_weight(w, fmt):
    k, n = w.shape
    w = f64(np.asarray(w, np.float32).astype(ml_dtypes.bfloat16)).reshape(k // 32, 32, n)
    amax = np.abs(w).max(1)
    if fmt == "e4m3":
        byte = np.frexp(amax)[1] - 1 + 127 - 7
    else:
        mant, ex = np.frexp(amax / 6.0)
        byte = np.where(mant > 0.5, ex, ex - 1) + 127
    byte = np.clip(np.where(amax > 0, byte, 1), 1, 254)
    scaled = (w * np.exp2(127.0 - byte)[:, None, :]).reshape(k, n).astype(np.float32)
    by_word = np.ascontiguousarray(scaled.reshape(k // 512, 128, 4, n).transpose(0, 1, 3, 2))
    if fmt == "e4m3":
        words = by_word.astype(ml_dtypes.float8_e4m3fn).view(np.uint8)
    else:
        c = by_word.astype(ml_dtypes.float4_e2m1fn).view(np.uint8) & 0xF
        words = (c[..., 0::2] | (c[..., 1::2] << 4)).reshape(k // 512, 128, 2 * n)
    return np.ascontiguousarray(words), np.ascontiguousarray(byte.astype(np.uint8).reshape(k // 512, 16, n))


def unpack_weight(words, scales, fmt):
    g, _, n = scales.shape
    words = np.ascontiguousarray(words).reshape(g, 128, n, -1)
    if fmt == "e4m3":
        vals = words.view(ml_dtypes.float8_e4m3fn).astype(np.float64)
    else:
        nib = np.empty((g, 128, n, 4), np.uint8)
        nib[..., 0::2] = words & 0xF
        nib[..., 1::2] = words >> 4
        vals = E2M1[nib]
    vals = vals * np.repeat(np.exp2(scales.astype(np.float64) - 127.0), 8, axis=1)[..., None]
    return vals.transpose(0, 1, 3, 2).reshape(g * 512, n)


def bf(x):
    return np.asarray(x, np.float32).astype(ml_dtypes.bfloat16)


def planes(Y):
    r, m = Y.shape
    b = f64(bf(Y)).reshape(r // 32, 32, m)
    amax = np.abs(b).max(1)
    byte = np.clip(np.where(amax > 0, np.frexp(amax)[1] - 1 + 127 - 7, 1), 1, 254)
    codes = (b * np.exp2(127.0 - byte)[:, None, :]).reshape(r, m).astype(np.float32).astype(ml_dtypes.float8_e4m3fn).view(np.uint8)
    words = codes.reshape(r // 512, 128, 4, m).transpose(0, 1, 3, 2)
    return np.ascontiguousarray(words), np.ascontiguousarray(byte.astype(np.uint8).reshape(r // 512, 16, m))


D, T, U, J, I = 512, 2048, 1024, 512, 512


def setup_inputs():
    n = np.random.standard_normal
    idx = np.stack([np.random.permutation(T)[:I] for _ in range(8)])
    idx2 = np.random.permutation(U)[:J]
    fd = mx_kscale(D)
    piecep = pack_weight(n((D, T)) / fd[:, None], "e4m3")
    return {
        "ent": (n((D, U)) * 1.2 / np.sqrt(D)).astype(np.float32),
        "fsc": (np.random.uniform(0.5, 1.5, (D, 1)) * fd[:, None]).astype(np.float32),
        "piece_words": piecep[0],
        "piece_scales": piecep[1],
        "steep": (np.random.uniform(0.5, 2.0, (J, 1))).astype(np.float32),
        "cwt": (np.random.uniform(0.5, 2.0, (1, I))).astype(np.float32),
        "bias": (0.3 * n((J, I))).astype(np.float32),
        "offs": striped8(idx),
        "offs2": striped(idx2),
    }


def reference(ent, fsc, piece_words, piece_scales, steep, cwt, bias, offs, offs2):
    idx = unstriped8(offs)
    idx2 = unstriped(offs2)
    pieceu = unpack_weight(piece_words, piece_scales, "e4m3")
    ex = f64(ent)[:, idx2] * f64(fsc)
    exq = mxq(ex, 0, "e4m3")
    pieceidxg = pick8(pieceu, idx, 64)
    a = exq.T @ pieceidxg
    y = np.tanh(a * f64(steep)) * f64(cwt) + f64(bias)
    words, scales = planes(y)
    return y, words, scales

@@ -1,0 +1,173 @@
+from contextlib import ExitStack
+
+import concourse.mybir as mybir
+from concourse.masks import make_identity
+
+D, T, U, J, I = 512, 2048, 1024, 512, 512
+FLOPS = 2 * D * J * I
+
+F32 = mybir.dt.float32
+BF16 = mybir.dt.bfloat16
+I32 = mybir.dt.int32
+U32 = mybir.dt.uint32
+U16 = mybir.dt.uint16
+U8 = mybir.dt.uint8
+FP8X4 = mybir.dt.float8_e4m3fn_x4
+ACT = mybir.ActivationFunctionType
+ALU = mybir.AluOpType
+
+P = 128
+PACK = 4
+CHUNK = 128
+NCHUNK = I // CHUNK
+HALF = I // 2
+
+
+def tile_attend_composedpairs_pl_kernel(tc, ent, fsc, piece_words, piece_scales, steep, cwt, bias, offs, offs2,
+                                         out_0, out_1, out_2):
+    nc = tc.nc
+    with ExitStack() as ctx:
+        keep = ctx.enter_context(tc.tile_pool(name="keep", bufs=1))
+        psum = ctx.enter_context(tc.psum_pool(name="psum", bufs=1))
+
+        offs_sb = keep.tile([P, I // 16], U16, name="offs_sb")
+        offs2_sb = keep.tile([P, J // 16], U16, name="offs2_sb")
+        nc.sync.dma_start(offs_sb[:], offs)
+        nc.sync.dma_start(offs2_sb[:], offs2)
+
+        sc_win = keep.tile([P, T], U8, name="sc_win", align_bytes=64)
+        nc.gpsimd.memset(sc_win[:].bitcast(I32), 0)
+        nc.gpsimd.dma_start(sc_win[0:P:8, :].bitcast(I32), piece_scales[0].bitcast(I32))
+
+        fsc_sb = keep.tile([P, PACK], F32, name="fsc_sb")
+        cwt_sb = keep.tile([P, PACK], F32, name="cwt_sb")
+        steep_sb = keep.tile([P, PACK], F32, name="steep_sb")
+        nc.scalar.dma_start(fsc_sb[:], fsc.rearrange("(p t) o -> p (t o)", t=PACK))
+        nc.scalar.dma_start(cwt_sb[:], cwt.rearrange("o (p t) -> (o p) t", t=PACK))
+        nc.scalar.dma_start(steep_sb[:], steep.rearrange("(p t) o -> p (t o)", t=PACK))
+
+        ent_rows = ent.rearrange("(p t) u -> p t u", t=PACK)
+        ent_win = []
+        for t in range(PACK):
+            w = keep.tile([P, U], F32, name="ent_win%d" % t)
+            nc.sync.dma_start(w[:], ent_rows[:, t, :])
+            ent_win.append(w)
+        word_win = keep.tile([P, T], U32, name="word_win", align_bytes=64)
+        nc.sync.dma_start(word_win[:].bitcast(I32), piece_words[0].rearrange("p n t -> p (n t)").bitcast(I32))
+        bias_sb = keep.tile([P, PACK, I], F32, name="bias_sb")
+        nc.sync.dma_start(bias_sb[:], bias.rearrange("(p t) i -> p t i", t=PACK))
+
+        ident = keep.tile([P, P], F32, name="ident")
+        make_identity(nc, ident[:])
+        piece_sc = keep.tile([P, I], U8, name="piece_sc", align_bytes=64)
+        nc.gpsimd.memset(piece_sc[:].bitcast(I32), 0)
+
+        warm = keep.tile([P, 1], F32, name="warm")
+        zero = keep.tile([P, 1], F32, name="zero")
+        nc.vector.memset(zero[:], 0.0)
+        nc.scalar.activation(warm[:], zero[:], ACT.Tanh)
+
+        sc_got = keep.tile([P, I], U8, name="sc_got", align_bytes=64)
+        nc.vector.tensor_copy(sc_got[:], sc_win[:].indirect(offs_sb[:]))
+        for r in range(4):
+            nc.scalar.dma_start(piece_sc[r:P:32, :].bitcast(I32), sc_got[8 * r:P:32, :].bitcast(I32))
+
+        cwt_ps = psum.tile([P, I], F32, name="cwt_ps")
+        for t in range(PACK):
+            nc.tensor.transpose(cwt_ps[:, t:I:PACK], cwt_sb[:, t:t + 1].to_broadcast([P, P]), ident[:])
+
+        pairs = keep.tile([P, 2, PACK, P, 2], BF16, name="pairs", align_bytes=64)
+        for t in range(PACK):
+            got = keep.tile([P, J], F32, name="ent_got%d" % t)
+            nc.vector.tensor_copy(got[:], ent_win[t][:].indirect(offs2_sb[:]))
+            nc.scalar.activation(pairs[:, t // 2, :, :, t % 2].rearrange("p r m -> p m r"),
+                                 got[:].rearrange("p (m r) -> p m r", r=PACK), ACT.Copy, scale=fsc_sb[:, t:t + 1])
+
+        piece_w = []
+        for h in range(2):
+            pw = keep.tile([P, HALF], U32, name="piece_w%d" % h, align_bytes=64)
+            piece_w.append(pw)
+        nc.vector.tensor_copy(piece_w[0][:], word_win[:].indirect(offs_sb[:, 0:16]))
+
+        pair_words = pairs[:].rearrange("p u r m e -> p u (r m e)").bitcast(F32)
+        ex_b = []
+        for h in range(2):
+            xb = keep.tile([P, HALF, PACK], BF16, name="ex_b%d" % h, align_bytes=64)
+            nc.vector.tensor_copy(xb[:].rearrange("p c t -> p (c t)").bitcast(F32).rearrange("p (c u) -> p c u", u=2),
+                                  pair_words[:, :, h * HALF:(h + 1) * HALF].rearrange("p u c -> p c u"))
+            ex_b.append(xb)
+        ex_w = keep.tile([P, J], U32, name="ex_w", align_bytes=64)
+        ex_sc = keep.tile([P, J], U8, name="ex_sc", align_bytes=64)
+        for h in range(2):
+            cols = slice(h * HALF, (h + 1) * HALF)
+            nc.vector.quantize_mx(out=ex_w[:, cols].bitcast(FP8X4), scales=ex_sc[:, cols],
+                                  in_=ex_b[h][:].rearrange("p c t -> p (c t)"))
+        nc.vector.tensor_copy(piece_w[1][:], word_win[:].indirect(offs_sb[:, 16:32]))
+
+        y_w = keep.tile([P, I], U32, name="y_w", align_bytes=64)
+        y_sc = keep.tile([P, I], U8, name="y_sc", align_bytes=64)
+        out_rows = out_0.rearrange("(p r) i -> p r i", r=PACK)
+        out_words = out_1[0].rearrange("p n t -> p (n t)").bitcast(I32)
+        out_scales = out_2[0].bitcast(I32)
+
+        th, prod, y, yb = [], [], [], []
+
+        def score(c):
+            acc = psum.tile([P, PACK, CHUNK], F32, name="acc%d" % c)
+            tile = keep.tile([P, PACK, CHUNK], F32, name="th%d" % c)
+            cols = slice(c * CHUNK, (c + 1) * CHUNK)
+            h, c0 = divmod(c * CHUNK, HALF)
+            for r in range(PACK):
+                rc = slice(r * P, (r + 1) * P)
+                nc.tensor.matmul_mx(out=acc[:, r, :], lhsT=ex_w[:, rc].bitcast(FP8X4), lhsT_scale=ex_sc[:, rc],
+                                    rhs=piece_w[h][:, c0:c0 + CHUNK].bitcast(FP8X4), rhs_scale=piece_sc[:, cols],
+                                    start=True, stop=True)
+            for r in range(PACK):
+                nc.scalar.activation(tile[:, r, :], acc[:, r, :], ACT.Tanh, scale=steep_sb[:, r:r + 1])
+            th.append(tile)
+
+        def weigh(c):
+            tile = keep.tile([P, PACK, CHUNK], F32, name="prod%d" % c)
+            cols = slice(c * CHUNK, (c + 1) * CHUNK)
+            nc.vector.tensor_tensor(tile[:], th[c][:], cwt_ps[:, cols].unsqueeze(1).to_broadcast([P, PACK, CHUNK]),
+                                    ALU.mult)
+            prod.append(tile)
+
+        def add_bias(c):
+            tile = keep.tile([P, PACK, CHUNK], F32, name="y%d" % c)
+            cols = slice(c * CHUNK, (c + 1) * CHUNK)
+            nc.vector.tensor_tensor(tile[:], prod[c][:], bias_sb[:, :, cols], ALU.add)
+            nc.sync.dma_start(out_rows[:, :, cols], tile[:])
+            y.append(tile)
+
+        def regroup(c):
+            tile = keep.tile([P, CHUNK, PACK], BF16, name="yb%d" % c, align_bytes=64)
+            src = y[c][:].rearrange("p r i -> p i r")
+            if c == NCHUNK - 1:
+                nc.vector.tensor_copy(tile[:], src)
+            else:
+                nc.scalar.copy(tile[:], src)
+            yb.append(tile)
+
+        def quantise(c):
+            cols = slice(c * CHUNK, (c + 1) * CHUNK)
+            nc.vector.quantize_mx(out=y_w[:, cols].bitcast(FP8X4), scales=y_sc[:, cols],
+                                  in_=yb[c][:].rearrange("p i r -> p (i r)"))
+
+        for c in range(NCHUNK):
+            score(c)
+        weigh(0)
+        for c in range(NCHUNK):
+            if c + 1 < NCHUNK:
+                weigh(c + 1)
+            add_bias(c)
+            regroup(c)
+            if c >= 1:
+                quantise(c - 1)
+            if c == 2:
+                nc.sync.dma_start(out_words[:, 0:HALF], y_w[:, 0:HALF].bitcast(I32))
+        quantise(NCHUNK - 1)
+        nc.sync.dma_start(out_words[:, HALF:I], y_w[:, HALF:I].bitcast(I32))
+        for q in range(4):
+            eng = nc.sync if q % 2 else nc.scalar
+            eng.dma_start(out_scales[4 * q:4 * q + 4, :], y_sc[32 * q:32 * q + 4, :].bitcast(I32))

@@ -18,9 +18,13 @@ ALU = mybir.AluOpType
 
 P = 128
 PACK = 4
-CHUNK = 128
-NCHUNK = I // CHUNK
-HALF = I // 2
+GROUP = 16
+BLOCKS = 16
+BLOCK_PARTS = 8
+QUAD = 32
+HALF = 256
+QUARTER = 128
+EIGHTH = 64
 
 
 def tile_attend_composedpairs_pl_kernel(tc, ent, fsc, piece_words, piece_scales, steep, cwt, bias, offs, offs2,
@@ -30,144 +34,169 @@ def tile_attend_composedpairs_pl_kernel(tc, ent, fsc, piece_words, piece_scales,
         keep = ctx.enter_context(tc.tile_pool(name="keep", bufs=1))
         psum = ctx.enter_context(tc.psum_pool(name="psum", bufs=1))
 
-        offs_sb = keep.tile([P, I // 16], U16, name="offs_sb")
-        offs2_sb = keep.tile([P, J // 16], U16, name="offs2_sb")
+        offs_sb = keep.tile([P, I // GROUP], U16, name="offs_sb")
+        offs2_sb = keep.tile([P, J // GROUP], U16, name="offs2_sb")
+        scale_store = keep.tile([P, T], U8, name="scale_store", tag="scale_store", align_bytes=64)
+        ent_planes = ent.rearrange("(p t) u -> p t u", t=PACK)
+        ent_sb = [keep.tile([P, U], F32, name="ent_sb%d" % t) for t in range(PACK)]
+        word_store = keep.tile([P, T], U32, name="word_store", align_bytes=64)
+        nc.sync.dma_start(scale_store[:].bitcast(I32),
+                          piece_scales[0].bitcast(I32).unsqueeze(1).to_broadcast([BLOCKS, BLOCK_PARTS, T // 4]))
         nc.sync.dma_start(offs_sb[:], offs)
+        nc.sync.dma_start(ent_sb[0][:], ent_planes[:, 0, :])
         nc.sync.dma_start(offs2_sb[:], offs2)
-
-        sc_win = keep.tile([P, T], U8, name="sc_win", align_bytes=64)
-        nc.gpsimd.memset(sc_win[:].bitcast(I32), 0)
-        nc.gpsimd.dma_start(sc_win[0:P:8, :].bitcast(I32), piece_scales[0].bitcast(I32))
+        for t in range(1, PACK):
+            nc.sync.dma_start(ent_sb[t][:], ent_planes[:, t, :])
+        nc.sync.dma_start(word_store[:].bitcast(I32), piece_words[0].rearrange("p n t -> p (n t)").bitcast(I32))
 
         fsc_sb = keep.tile([P, PACK], F32, name="fsc_sb")
-        cwt_sb = keep.tile([P, PACK], F32, name="cwt_sb")
         steep_sb = keep.tile([P, PACK], F32, name="steep_sb")
         nc.scalar.dma_start(fsc_sb[:], fsc.rearrange("(p t) o -> p (t o)", t=PACK))
-        nc.scalar.dma_start(cwt_sb[:], cwt.rearrange("o (p t) -> (o p) t", t=PACK))
-        nc.scalar.dma_start(steep_sb[:], steep.rearrange("(p t) o -> p (t o)", t=PACK))
+        nc.scalar.dma_start(steep_sb[:], steep.rearrange("(p r) o -> p (r o)", r=PACK))
 
-        ent_rows = ent.rearrange("(p t) u -> p t u", t=PACK)
-        ent_win = []
-        for t in range(PACK):
-            w = keep.tile([P, U], F32, name="ent_win%d" % t)
-            nc.sync.dma_start(w[:], ent_rows[:, t, :])
-            ent_win.append(w)
-        word_win = keep.tile([P, T], U32, name="word_win", align_bytes=64)
-        nc.sync.dma_start(word_win[:].bitcast(I32), piece_words[0].rearrange("p n t -> p (n t)").bitcast(I32))
-        bias_sb = keep.tile([P, PACK, I], F32, name="bias_sb")
-        nc.sync.dma_start(bias_sb[:], bias.rearrange("(p t) i -> p t i", t=PACK))
-
+        piece_scale = keep.tile([P, I], U8, name="piece_scale", align_bytes=64)
+        nc.gpsimd.memset(piece_scale[:].bitcast(I32), 0)
         ident = keep.tile([P, P], F32, name="ident")
         make_identity(nc, ident[:])
-        piece_sc = keep.tile([P, I], U8, name="piece_sc", align_bytes=64)
-        nc.gpsimd.memset(piece_sc[:].bitcast(I32), 0)
 
-        warm = keep.tile([P, 1], F32, name="warm")
-        zero = keep.tile([P, 1], F32, name="zero")
-        nc.vector.memset(zero[:], 0.0)
-        nc.scalar.activation(warm[:], zero[:], ACT.Tanh)
+        warm_in = keep.tile([P, 1], F32, name="warm_in")
+        warm_out = keep.tile([P, 1], F32, name="warm_out")
+        nc.vector.memset(warm_in[:], 0.0)
+        nc.scalar.activation(warm_out[:], warm_in[:], ACT.Tanh)
 
-        sc_got = keep.tile([P, I], U8, name="sc_got", align_bytes=64)
-        nc.vector.tensor_copy(sc_got[:], sc_win[:].indirect(offs_sb[:]))
-        for r in range(4):
-            nc.scalar.dma_start(piece_sc[r:P:32, :].bitcast(I32), sc_got[8 * r:P:32, :].bitcast(I32))
+        scale_got = keep.tile([P, I], U8, name="scale_got", align_bytes=64)
+        nc.vector.tensor_copy(scale_got[:], scale_store[:].indirect(offs_sb[:]))
+        for row in range(QUAD // BLOCK_PARTS):
+            nc.scalar.dma_start(piece_scale[row:P:QUAD, :].bitcast(I32),
+                                scale_got[BLOCK_PARTS * row:P:QUAD, :].bitcast(I32))
 
-        cwt_ps = psum.tile([P, I], F32, name="cwt_ps")
-        for t in range(PACK):
-            nc.tensor.transpose(cwt_ps[:, t:I:PACK], cwt_sb[:, t:t + 1].to_broadcast([P, P]), ident[:])
+        cwt_sb = keep.tile([P, PACK], F32, name="cwt_sb", tag="scale_store", align_bytes=64)
+        nc.sync.dma_start(cwt_sb[:], cwt.rearrange("o (p c) -> (o p) c", c=PACK))
+        cwt_row = psum.tile([P, I], F32, name="cwt_row")
+        for c in range(PACK):
+            nc.tensor.transpose(cwt_row[:, c:I:PACK], cwt_sb[:, c:c + 1].to_broadcast([P, P]), ident[:])
 
-        pairs = keep.tile([P, 2, PACK, P, 2], BF16, name="pairs", align_bytes=64)
-        for t in range(PACK):
-            got = keep.tile([P, J], F32, name="ent_got%d" % t)
-            nc.vector.tensor_copy(got[:], ent_win[t][:].indirect(offs2_sb[:]))
-            nc.scalar.activation(pairs[:, t // 2, :, :, t % 2].rearrange("p r m -> p m r"),
-                                 got[:].rearrange("p (m r) -> p m r", r=PACK), ACT.Copy, scale=fsc_sb[:, t:t + 1])
+        pairs = [keep.tile([P, 2, HALF, 2], BF16, name="pairs%d" % h, align_bytes=64) for h in range(2)]
 
-        piece_w = []
+        def scale_plane(t, h, got):
+            nc.scalar.activation(pairs[h][:, t // 2, :, t % 2], got, ACT.Copy, scale=fsc_sb[:, t:t + 1])
+
+        for t in range(PACK - 1):
+            got = keep.tile([P, J], F32, name="ent_got%d" % t, tag="ent_got%d" % t)
+            nc.vector.tensor_copy(got[:], ent_sb[t][:].indirect(offs2_sb[:]))
+            for h in range(2):
+                scale_plane(t, h, got[:, h * HALF:(h + 1) * HALF])
+
+        bias_rows = bias.rearrange("(p r) i -> p r i", r=PACK)
+        bias_sb = keep.tile([P, PACK, I], F32, name="bias_sb", tag="ent_got0")
+        for k in range(2):
+            nc.sync.dma_start(bias_sb[:, 2 * k:2 * k + 2, :], bias_rows[:, 2 * k:2 * k + 2, :])
+
+        ex_bf = [keep.tile([P, 2 * P * PACK], BF16, name="ex_bf%d" % k, tag="ex_bf%d" % k, align_bytes=64)
+                 for k in range(2)]
         for h in range(2):
-            pw = keep.tile([P, HALF], U32, name="piece_w%d" % h, align_bytes=64)
-            piece_w.append(pw)
-        nc.vector.tensor_copy(piece_w[0][:], word_win[:].indirect(offs_sb[:, 0:16]))
+            got = keep.tile([P, HALF], F32, name="ent_last%d" % h)
+            entries = slice(h * HALF // GROUP, (h + 1) * HALF // GROUP)
+            nc.vector.tensor_copy(got[:], ent_sb[PACK - 1][:].indirect(offs2_sb[:, entries]))
+            scale_plane(PACK - 1, h, got[:])
+            src = pairs[h][:].rearrange("p u j e -> p u (j e)").bitcast(F32)
+            src = src.rearrange("p u (n e r) -> p n r e u", e=2, r=PACK)
+            for k in range(2):
+                dst = ex_bf[k][:].bitcast(F32).rearrange("p (s h n e u) -> p h n s e u", s=2, h=2, e=2, u=2)
+                nc.scalar.copy(dst[:, h], src[:, :, 2 * k:2 * k + 2])
 
-        pair_words = pairs[:].rearrange("p u r m e -> p u (r m e)").bitcast(F32)
-        ex_b = []
-        for h in range(2):
-            xb = keep.tile([P, HALF, PACK], BF16, name="ex_b%d" % h, align_bytes=64)
-            nc.vector.tensor_copy(xb[:].rearrange("p c t -> p (c t)").bitcast(F32).rearrange("p (c u) -> p c u", u=2),
-                                  pair_words[:, :, h * HALF:(h + 1) * HALF].rearrange("p u c -> p c u"))
-            ex_b.append(xb)
-        ex_w = keep.tile([P, J], U32, name="ex_w", align_bytes=64)
-        ex_sc = keep.tile([P, J], U8, name="ex_sc", align_bytes=64)
-        for h in range(2):
-            cols = slice(h * HALF, (h + 1) * HALF)
-            nc.vector.quantize_mx(out=ex_w[:, cols].bitcast(FP8X4), scales=ex_sc[:, cols],
-                                  in_=ex_b[h][:].rearrange("p c t -> p (c t)"))
-        nc.vector.tensor_copy(piece_w[1][:], word_win[:].indirect(offs_sb[:, 16:32]))
+        piece_w = [keep.tile([P, HALF], U32, name="piece_w0", align_bytes=64)]
+        nc.vector.tensor_copy(piece_w[0][:], word_store[:].indirect(offs_sb[:, 0:HALF // GROUP]))
+        ex_words = keep.tile([P, J], U32, name="ex_words", tag="scale_store", align_bytes=64)
+        ex_scale = [keep.tile([P, P], U8, name="ex_scale%d" % r, align_bytes=64) for r in range(PACK)]
+        for r in range(PACK):
+            k, s = divmod(r, 2)
+            nc.vector.quantize_mx(out=ex_words[:, r * P:(r + 1) * P].bitcast(FP8X4), scales=ex_scale[r][:],
+                                  in_=ex_bf[k][:, s * P * PACK:(s + 1) * P * PACK])
+        piece_w.append(keep.tile([P, HALF], U32, name="piece_w1", tag="ex_bf1", align_bytes=64))
+        nc.vector.tensor_copy(piece_w[1][:], word_store[:].indirect(offs_sb[:, HALF // GROUP:I // GROUP]))
 
-        y_w = keep.tile([P, I], U32, name="y_w", align_bytes=64)
-        y_sc = keep.tile([P, I], U8, name="y_sc", align_bytes=64)
+        steps = [(0, slice(0, QUARTER)), (0, slice(QUARTER, HALF))] + [(r, slice(0, HALF)) for r in range(1, PACK)]
+        acc_second = [psum.tile([P, 2, HALF], F32, name="acc_second%d" % k) for k in range(2)]
+        th = [keep.tile([P, PACK, HALF], F32, name="th%d" % h) for h in range(2)]
+
+        def product(r, h, part, acc):
+            cols = slice(h * HALF + part.start, h * HALF + part.stop)
+            nc.tensor.matmul_mx(out=acc, lhsT=ex_words[:, r * P:(r + 1) * P].bitcast(FP8X4), lhsT_scale=ex_scale[r][:],
+                                rhs=piece_w[h][:, part].bitcast(FP8X4), rhs_scale=piece_scale[:, cols],
+                                start=True, stop=True)
+
+        def squash(r, h, part, acc):
+            nc.scalar.activation(th[h][:, r, part], acc, ACT.Tanh, scale=steep_sb[:, r:r + 1])
+
+        first = slice(0, HALF)
+        for n, (r, part) in enumerate(steps):
+            acc = psum.tile([P, part.stop - part.start], F32, name="acc_first%d" % n)
+            product(r, 0, part, acc[:])
+            squash(r, 0, part, acc[:])
+        for k in range(2):
+            for s in range(2):
+                product(2 * k + s, 1, first, acc_second[k][:, s, :])
+            for s in range(2):
+                squash(2 * k + s, 1, first, acc_second[k][:, s, :])
+
+        y_words = keep.tile([P, I], U32, name="y_words", align_bytes=64)
+        y_scale = keep.tile([P, I], U8, name="y_scale", align_bytes=64)
         out_rows = out_0.rearrange("(p r) i -> p r i", r=PACK)
         out_words = out_1[0].rearrange("p n t -> p (n t)").bitcast(I32)
         out_scales = out_2[0].bitcast(I32)
 
-        th, prod, y, yb = [], [], [], []
+        def regroup(copy, y_bf, y):
+            copy(y_bf.rearrange("p (c i r) -> p c r i", i=4, r=PACK), y.rearrange("p r (c i) -> p c r i", i=4))
 
-        def score(c):
-            acc = psum.tile([P, PACK, CHUNK], F32, name="acc%d" % c)
-            tile = keep.tile([P, PACK, CHUNK], F32, name="th%d" % c)
-            cols = slice(c * CHUNK, (c + 1) * CHUNK)
-            h, c0 = divmod(c * CHUNK, HALF)
-            for r in range(PACK):
-                rc = slice(r * P, (r + 1) * P)
-                nc.tensor.matmul_mx(out=acc[:, r, :], lhsT=ex_w[:, rc].bitcast(FP8X4), lhsT_scale=ex_sc[:, rc],
-                                    rhs=piece_w[h][:, c0:c0 + CHUNK].bitcast(FP8X4), rhs_scale=piece_sc[:, cols],
-                                    start=True, stop=True)
-            for r in range(PACK):
-                nc.scalar.activation(tile[:, r, :], acc[:, r, :], ACT.Tanh, scale=steep_sb[:, r:r + 1])
-            th.append(tile)
+        def quantise(y_bf, cols):
+            nc.vector.quantize_mx(out=y_words[:, cols].bitcast(FP8X4), scales=y_scale[:, cols], in_=y_bf[:])
 
-        def weigh(c):
-            tile = keep.tile([P, PACK, CHUNK], F32, name="prod%d" % c)
-            cols = slice(c * CHUNK, (c + 1) * CHUNK)
-            nc.vector.tensor_tensor(tile[:], th[c][:], cwt_ps[:, cols].unsqueeze(1).to_broadcast([P, PACK, CHUNK]),
-                                    ALU.mult)
-            prod.append(tile)
+        prod_first = keep.tile([P, PACK, HALF], F32, name="prod_first")
+        y_first = keep.tile([P, PACK, HALF], F32, name="y_first")
 
-        def add_bias(c):
-            tile = keep.tile([P, PACK, CHUNK], F32, name="y%d" % c)
-            cols = slice(c * CHUNK, (c + 1) * CHUNK)
-            nc.vector.tensor_tensor(tile[:], prod[c][:], bias_sb[:, :, cols], ALU.add)
-            nc.sync.dma_start(out_rows[:, :, cols], tile[:])
-            y.append(tile)
+        def add_first(r):
+            nc.vector.tensor_tensor(y_first[:, r, :], prod_first[:, r, :], bias_sb[:, r, first], ALU.add)
+            if r % 2 == 1:
+                nc.sync.dma_start(out_rows[:, r - 1:r + 1, first], y_first[:, r - 1:r + 1, :])
 
-        def regroup(c):
-            tile = keep.tile([P, CHUNK, PACK], BF16, name="yb%d" % c, align_bytes=64)
-            src = y[c][:].rearrange("p r i -> p i r")
-            if c == NCHUNK - 1:
-                nc.vector.tensor_copy(tile[:], src)
-            else:
-                nc.scalar.copy(tile[:], src)
-            yb.append(tile)
+        for r, part in steps:
+            nc.vector.tensor_tensor(prod_first[:, r, part], th[0][:, r, part], cwt_row[:, part], ALU.mult)
+            if r > 0:
+                add_first(r - 1)
+        add_first(PACK - 1)
+        y_bf_first = keep.tile([P, HALF * PACK], BF16, name="y_bf_first", align_bytes=64)
+        regroup(nc.scalar.copy, y_bf_first[:], y_first[:])
 
-        def quantise(c):
-            cols = slice(c * CHUNK, (c + 1) * CHUNK)
-            nc.vector.quantize_mx(out=y_w[:, cols].bitcast(FP8X4), scales=y_sc[:, cols],
-                                  in_=yb[c][:].rearrange("p i r -> p (i r)"))
+        third, fourth = slice(HALF, HALF + QUARTER), slice(HALF + QUARTER, I)
+        prod_second = keep.tile([P, PACK, HALF], F32, name="prod_second")
+        for c, cols in enumerate((third, fourth)):
+            part = slice(c * QUARTER, (c + 1) * QUARTER)
+            nc.vector.tensor_tensor(prod_second[:, :, part], th[1][:, :, part],
+                                    cwt_row[:, cols].unsqueeze(1).to_broadcast([P, PACK, QUARTER]), ALU.mult)
 
-        for c in range(NCHUNK):
-            score(c)
-        weigh(0)
-        for c in range(NCHUNK):
-            if c + 1 < NCHUNK:
-                weigh(c + 1)
-            add_bias(c)
-            regroup(c)
-            if c >= 1:
-                quantise(c - 1)
-            if c == 2:
-                nc.sync.dma_start(out_words[:, 0:HALF], y_w[:, 0:HALF].bitcast(I32))
-        quantise(NCHUNK - 1)
-        nc.sync.dma_start(out_words[:, HALF:I], y_w[:, HALF:I].bitcast(I32))
-        for q in range(4):
-            eng = nc.sync if q % 2 else nc.scalar
-            eng.dma_start(out_scales[4 * q:4 * q + 4, :], y_sc[32 * q:32 * q + 4, :].bitcast(I32))
+        y_third = keep.tile([P, PACK, QUARTER], F32, name="y_third")
+        y_bf_third = keep.tile([P, QUARTER * PACK], BF16, name="y_bf_third", align_bytes=64)
+        nc.vector.tensor_tensor(y_third[:], prod_second[:, :, 0:QUARTER], bias_sb[:, :, third], ALU.add)
+        nc.sync.dma_start(out_rows[:, :, third], y_third[:])
+        regroup(nc.scalar.copy, y_bf_third[:], y_third[:])
+
+        y_fourth = keep.tile([P, PACK, QUARTER], F32, name="y_fourth")
+        y_bf_fourth = keep.tile([P, QUARTER * PACK], BF16, name="y_bf_fourth", align_bytes=64)
+        for e in range(2):
+            c0 = e * EIGHTH
+            nc.vector.tensor_tensor(y_fourth[:, :, c0:c0 + EIGHTH],
+                                    prod_second[:, :, QUARTER + c0:QUARTER + c0 + EIGHTH],
+                                    bias_sb[:, :, fourth.start + c0:fourth.start + c0 + EIGHTH], ALU.add)
+        nc.sync.dma_start(out_rows[:, :, fourth], y_fourth[:])
+        regroup(nc.scalar.copy, y_bf_fourth[:, 0:EIGHTH * PACK], y_fourth[:, :, 0:EIGHTH])
+        quantise(y_bf_first, first)
+        nc.sync.dma_start(out_words[:, first], y_words[:, first].bitcast(I32))
+        regroup(nc.vector.tensor_copy, y_bf_fourth[:, EIGHTH * PACK:QUARTER * PACK], y_fourth[:, :, EIGHTH:QUARTER])
+        quantise(y_bf_third, third)
+        quantise(y_bf_fourth, fourth)
+
+        nc.sync.dma_start(out_words[:, HALF:I], y_words[:, HALF:I].bitcast(I32))
+        for x in range(P // QUAD):
+            queue = nc.sync if x % 2 else nc.scalar
+            queue.dma_start(out_scales[4 * x:4 * x + 4, :], y_scale[QUAD * x:QUAD * x + 4, :].bitcast(I32))

from contextlib import ExitStack

import concourse.mybir as mybir
from concourse.masks import make_identity

D, T, U, J, I = 512, 2048, 1024, 512, 512
FLOPS = 2 * D * J * I

F32 = mybir.dt.float32
BF16 = mybir.dt.bfloat16
I32 = mybir.dt.int32
U32 = mybir.dt.uint32
U16 = mybir.dt.uint16
U8 = mybir.dt.uint8
FP8X4 = mybir.dt.float8_e4m3fn_x4
ACT = mybir.ActivationFunctionType
ALU = mybir.AluOpType

P = 128
PACK = 4
GROUP = 16
BLOCKS = 16
BLOCK_PARTS = 8
QUAD = 32
HALF = 256
QUARTER = 128
EIGHTH = 64


def tile_attend_composedpairs_pl_kernel(tc, ent, fsc, piece_words, piece_scales, steep, cwt, bias, offs, offs2,
                                         out_0, out_1, out_2):
    nc = tc.nc
    with ExitStack() as ctx:
        keep = ctx.enter_context(tc.tile_pool(name="keep", bufs=1))
        psum = ctx.enter_context(tc.psum_pool(name="psum", bufs=1))

        offs_sb = keep.tile([P, I // GROUP], U16, name="offs_sb")
        offs2_sb = keep.tile([P, J // GROUP], U16, name="offs2_sb")
        scale_store = keep.tile([P, T], U8, name="scale_store", tag="scale_store", align_bytes=64)
        ent_planes = ent.rearrange("(p t) u -> p t u", t=PACK)
        ent_sb = [keep.tile([P, U], F32, name="ent_sb%d" % t) for t in range(PACK)]
        word_store = keep.tile([P, T], U32, name="word_store", align_bytes=64)
        nc.sync.dma_start(scale_store[:].bitcast(I32),
                          piece_scales[0].bitcast(I32).unsqueeze(1).to_broadcast([BLOCKS, BLOCK_PARTS, T // 4]))
        nc.sync.dma_start(offs_sb[:], offs)
        nc.sync.dma_start(ent_sb[0][:], ent_planes[:, 0, :])
        nc.sync.dma_start(offs2_sb[:], offs2)
        for t in range(1, PACK):
            nc.sync.dma_start(ent_sb[t][:], ent_planes[:, t, :])
        nc.sync.dma_start(word_store[:].bitcast(I32), piece_words[0].rearrange("p n t -> p (n t)").bitcast(I32))

        fsc_sb = keep.tile([P, PACK], F32, name="fsc_sb")
        steep_sb = keep.tile([P, PACK], F32, name="steep_sb")
        nc.scalar.dma_start(fsc_sb[:], fsc.rearrange("(p t) o -> p (t o)", t=PACK))
        nc.scalar.dma_start(steep_sb[:], steep.rearrange("(p r) o -> p (r o)", r=PACK))

        piece_scale = keep.tile([P, I], U8, name="piece_scale", align_bytes=64)
        nc.gpsimd.memset(piece_scale[:].bitcast(I32), 0)
        ident = keep.tile([P, P], F32, name="ident")
        make_identity(nc, ident[:])

        warm_in = keep.tile([P, 1], F32, name="warm_in")
        warm_out = keep.tile([P, 1], F32, name="warm_out")
        nc.vector.memset(warm_in[:], 0.0)
        nc.scalar.activation(warm_out[:], warm_in[:], ACT.Tanh)

        scale_got = keep.tile([P, I], U8, name="scale_got", align_bytes=64)
        nc.vector.tensor_copy(scale_got[:], scale_store[:].indirect(offs_sb[:]))
        for row in range(QUAD // BLOCK_PARTS):
            nc.scalar.dma_start(piece_scale[row:P:QUAD, :].bitcast(I32),
                                scale_got[BLOCK_PARTS * row:P:QUAD, :].bitcast(I32))

        cwt_sb = keep.tile([P, PACK], F32, name="cwt_sb", tag="scale_store", align_bytes=64)
        nc.sync.dma_start(cwt_sb[:], cwt.rearrange("o (p c) -> (o p) c", c=PACK))
        cwt_row = psum.tile([P, I], F32, name="cwt_row")
        for c in range(PACK):
            nc.tensor.transpose(cwt_row[:, c:I:PACK], cwt_sb[:, c:c + 1].to_broadcast([P, P]), ident[:])

        pairs = [keep.tile([P, 2, HALF, 2], BF16, name="pairs%d" % h, align_bytes=64) for h in range(2)]

        def scale_plane(t, h, got):
            nc.scalar.activation(pairs[h][:, t // 2, :, t % 2], got, ACT.Copy, scale=fsc_sb[:, t:t + 1])

        for t in range(PACK - 1):
            got = keep.tile([P, J], F32, name="ent_got%d" % t, tag="ent_got%d" % t)
            nc.vector.tensor_copy(got[:], ent_sb[t][:].indirect(offs2_sb[:]))
            for h in range(2):
                scale_plane(t, h, got[:, h * HALF:(h + 1) * HALF])

        bias_rows = bias.rearrange("(p r) i -> p r i", r=PACK)
        bias_sb = keep.tile([P, PACK, I], F32, name="bias_sb", tag="ent_got0")
        for k in range(2):
            nc.sync.dma_start(bias_sb[:, 2 * k:2 * k + 2, :], bias_rows[:, 2 * k:2 * k + 2, :])

        ex_bf = [keep.tile([P, 2 * P * PACK], BF16, name="ex_bf%d" % k, tag="ex_bf%d" % k, align_bytes=64)
                 for k in range(2)]
        for h in range(2):
            got = keep.tile([P, HALF], F32, name="ent_last%d" % h)
            entries = slice(h * HALF // GROUP, (h + 1) * HALF // GROUP)
            nc.vector.tensor_copy(got[:], ent_sb[PACK - 1][:].indirect(offs2_sb[:, entries]))
            scale_plane(PACK - 1, h, got[:])
            src = pairs[h][:].rearrange("p u j e -> p u (j e)").bitcast(F32)
            src = src.rearrange("p u (n e r) -> p n r e u", e=2, r=PACK)
            for k in range(2):
                dst = ex_bf[k][:].bitcast(F32).rearrange("p (s h n e u) -> p h n s e u", s=2, h=2, e=2, u=2)
                nc.scalar.copy(dst[:, h], src[:, :, 2 * k:2 * k + 2])

        piece_w = [keep.tile([P, HALF], U32, name="piece_w0", align_bytes=64)]
        nc.vector.tensor_copy(piece_w[0][:], word_store[:].indirect(offs_sb[:, 0:HALF // GROUP]))
        ex_words = keep.tile([P, J], U32, name="ex_words", tag="scale_store", align_bytes=64)
        ex_scale = [keep.tile([P, P], U8, name="ex_scale%d" % r, align_bytes=64) for r in range(PACK)]
        for r in range(PACK):
            k, s = divmod(r, 2)
            nc.vector.quantize_mx(out=ex_words[:, r * P:(r + 1) * P].bitcast(FP8X4), scales=ex_scale[r][:],
                                  in_=ex_bf[k][:, s * P * PACK:(s + 1) * P * PACK])
        piece_w.append(keep.tile([P, HALF], U32, name="piece_w1", tag="ex_bf1", align_bytes=64))
        nc.vector.tensor_copy(piece_w[1][:], word_store[:].indirect(offs_sb[:, HALF // GROUP:I // GROUP]))

        steps = [(0, slice(0, QUARTER)), (0, slice(QUARTER, HALF))] + [(r, slice(0, HALF)) for r in range(1, PACK)]
        acc_second = [psum.tile([P, 2, HALF], F32, name="acc_second%d" % k) for k in range(2)]
        th = [keep.tile([P, PACK, HALF], F32, name="th%d" % h) for h in range(2)]

        def product(r, h, part, acc):
            cols = slice(h * HALF + part.start, h * HALF + part.stop)
            nc.tensor.matmul_mx(out=acc, lhsT=ex_words[:, r * P:(r + 1) * P].bitcast(FP8X4), lhsT_scale=ex_scale[r][:],
                                rhs=piece_w[h][:, part].bitcast(FP8X4), rhs_scale=piece_scale[:, cols],
                                start=True, stop=True)

        def squash(r, h, part, acc):
            nc.scalar.activation(th[h][:, r, part], acc, ACT.Tanh, scale=steep_sb[:, r:r + 1])

        first = slice(0, HALF)
        for n, (r, part) in enumerate(steps):
            acc = psum.tile([P, part.stop - part.start], F32, name="acc_first%d" % n)
            product(r, 0, part, acc[:])
            squash(r, 0, part, acc[:])
        for k in range(2):
            for s in range(2):
                product(2 * k + s, 1, first, acc_second[k][:, s, :])
            for s in range(2):
                squash(2 * k + s, 1, first, acc_second[k][:, s, :])

        y_words = keep.tile([P, I], U32, name="y_words", align_bytes=64)
        y_scale = keep.tile([P, I], U8, name="y_scale", align_bytes=64)
        out_rows = out_0.rearrange("(p r) i -> p r i", r=PACK)
        out_words = out_1[0].rearrange("p n t -> p (n t)").bitcast(I32)
        out_scales = out_2[0].bitcast(I32)

        def regroup(copy, y_bf, y):
            copy(y_bf.rearrange("p (c i r) -> p c r i", i=4, r=PACK), y.rearrange("p r (c i) -> p c r i", i=4))

        def quantise(y_bf, cols):
            nc.vector.quantize_mx(out=y_words[:, cols].bitcast(FP8X4), scales=y_scale[:, cols], in_=y_bf[:])

        prod_first = keep.tile([P, PACK, HALF], F32, name="prod_first")
        y_first = keep.tile([P, PACK, HALF], F32, name="y_first")

        def add_first(r):
            nc.vector.tensor_tensor(y_first[:, r, :], prod_first[:, r, :], bias_sb[:, r, first], ALU.add)
            if r % 2 == 1:
                nc.sync.dma_start(out_rows[:, r - 1:r + 1, first], y_first[:, r - 1:r + 1, :])

        for r, part in steps:
            nc.vector.tensor_tensor(prod_first[:, r, part], th[0][:, r, part], cwt_row[:, part], ALU.mult)
            if r > 0:
                add_first(r - 1)
        add_first(PACK - 1)
        y_bf_first = keep.tile([P, HALF * PACK], BF16, name="y_bf_first", align_bytes=64)
        regroup(nc.scalar.copy, y_bf_first[:], y_first[:])

        third, fourth = slice(HALF, HALF + QUARTER), slice(HALF + QUARTER, I)
        prod_second = keep.tile([P, PACK, HALF], F32, name="prod_second")
        for c, cols in enumerate((third, fourth)):
            part = slice(c * QUARTER, (c + 1) * QUARTER)
            nc.vector.tensor_tensor(prod_second[:, :, part], th[1][:, :, part],
                                    cwt_row[:, cols].unsqueeze(1).to_broadcast([P, PACK, QUARTER]), ALU.mult)

        y_third = keep.tile([P, PACK, QUARTER], F32, name="y_third")
        y_bf_third = keep.tile([P, QUARTER * PACK], BF16, name="y_bf_third", align_bytes=64)
        nc.vector.tensor_tensor(y_third[:], prod_second[:, :, 0:QUARTER], bias_sb[:, :, third], ALU.add)
        nc.sync.dma_start(out_rows[:, :, third], y_third[:])
        regroup(nc.scalar.copy, y_bf_third[:], y_third[:])

        y_fourth = keep.tile([P, PACK, QUARTER], F32, name="y_fourth")
        y_bf_fourth = keep.tile([P, QUARTER * PACK], BF16, name="y_bf_fourth", align_bytes=64)
        for e in range(2):
            c0 = e * EIGHTH
            nc.vector.tensor_tensor(y_fourth[:, :, c0:c0 + EIGHTH],
                                    prod_second[:, :, QUARTER + c0:QUARTER + c0 + EIGHTH],
                                    bias_sb[:, :, fourth.start + c0:fourth.start + c0 + EIGHTH], ALU.add)
        nc.sync.dma_start(out_rows[:, :, fourth], y_fourth[:])
        regroup(nc.scalar.copy, y_bf_fourth[:, 0:EIGHTH * PACK], y_fourth[:, :, 0:EIGHTH])
        quantise(y_bf_first, first)
        nc.sync.dma_start(out_words[:, first], y_words[:, first].bitcast(I32))
        regroup(nc.vector.tensor_copy, y_bf_fourth[:, EIGHTH * PACK:QUARTER * PACK], y_fourth[:, :, EIGHTH:QUARTER])
        quantise(y_bf_third, third)
        quantise(y_bf_fourth, fourth)

        nc.sync.dma_start(out_words[:, HALF:I], y_words[:, HALF:I].bitcast(I32))
        for x in range(P // QUAD):
            queue = nc.sync if x % 2 else nc.scalar
            queue.dma_start(out_scales[4 * x:4 * x + 4, :], y_scale[QUAD * x:QUAD * x + 4, :].bitcast(I32))
